import numpy as np, ml_dtypes
CORES = [3,7,11,15,131,135,139,143]
N = 8
import mx_ref
NC, GR, GC, KT = 128, 2, 4, 1
TS = GC * KT
CH = GR * NC // GC
BF = ml_dtypes.bfloat16
def setup_inputs(rng):
    def f(*shape):
        return mx_ref.flush((rng.standard_normal(shape, dtype=np.float32) * np.exp2(rng.integers(-2, 3, shape[:-1] + (1,)))).astype(BF))
    return {"w": f(N, 128, KT * 512), "x": f(N, 128, KT * 4 * NC)}
def setup_inputs_blocks(rng):
    d = setup_inputs(rng)
    for k in ("w", "x"): d[k] = mx_ref.spread(d[k], rng, 1)
    return d
def setup_inputs_wide(rng):
    d = setup_inputs(rng)
    for k in ("w", "x"): d[k] = mx_ref.flush((d[k].astype(np.float32) * np.exp2(rng.integers(-8, 9, (N, 1, 1))).astype(np.float32)).astype(BF))
    return d
def setup_inputs_zeros(rng):
    d = setup_inputs(rng); v = d["x"].reshape(N, 128, -1, 4).copy()
    v[np.broadcast_to((rng.random((N, 1, v.shape[2], 1)) < 0.33), v.shape)] = 0
    d["x"] = v.reshape(d["x"].shape)
    return d
def reference(w, x):
    QX = [[mx_ref.quantize(x[r][:, 4 * NC * t:4 * NC * t + 4 * NC]) for t in range(KT)] for r in range(N)]
    y = np.zeros((N, 128, CH), np.float32)
    for i in range(GR):
        for s in range(TS):
            k, t = s // KT, s % KT
            qw = mx_ref.quantize(w[i * GC + k][:, 512 * t:512 * t + 512])
            p = np.concatenate([mx_ref.matmul(qw, QX[g * GC + k][t]) for g in range(GR)], axis=1)
            Y = p if s == 0 else Y + p
        for c in range(GC):
            y[i * GC + c] = Y[:, CH * c:CH * c + CH]
    return {"y": y}

from concourse.bass import DstId, RemoteDMATransfer
from concourse.mybir import dt, AluOpType

GR, GC, NC = 2, 4, 128
CH = GR * NC // GC

SCRATCH = {
    "xb": ("sbuf", [128, 4 * NC], "bfloat16"),
    "wb": ("sbuf", [128, 512], "bfloat16"),
    "xq": ("sbuf", [128, NC], "float8_e4m3fn_x4"),
    "xs": ("sbuf", [128, NC], "uint8"),
    "wq": ("sbuf", [128, 128], "float8_e4m3fn_x4"),
    "ws": ("sbuf", [128, 128], "uint8"),
    "rq": ("sbuf", [128, NC], "float8_e4m3fn_x4"),
    "rs": ("sbuf", [128, NC], "uint8"),
    "pl": ("psum", [128, 512], "float32"),
    "pc": ("psum", [128, 512], "float32"),
    "sl": ("sbuf", [128, NC], "float32"),
    "sc": ("sbuf", [128, NC], "float32"),
    "land": ("sbuf", [128, (GC - 1) * CH], "float32"),
    "yb": ("sbuf", [128, CH], "float32"),
}
SEMAPHORES = ["lx", "lw", "ly", "qx", "qw", "ml", "mc", "cl", "cc", "xa", "p0", "p1", "p2", "va", "sent"]


def _bits(mask):
    return [b for b in range(mask.bit_length()) if (mask >> b) & 1]


def _plan(r, cores, topo):
    row, col = r // GC, r % GC
    peer = (GR - 1 - row) * GC + col
    owners = {}
    for gx in range(GR):
        owners[gx] = [(row * GC + (gx * NC) // CH + j, j) for j in range(NC // CH)]
        owners[gx] = [(d, j) for d, j in owners[gx] if d != r]
    pool = topo.mask(cores[r], cores[peer])
    for gx in range(GR):
        for d, _ in owners[gx]:
            pool &= topo.mask(cores[r], cores[d])
    eng = _bits(pool)
    parts = {}
    for gx in range(GR):
        n = len(eng) // len(owners[gx])
        parts[gx] = [(d, j, sum(1 << b for b in eng[t * n:(t + 1) * n])) for t, (d, j) in enumerate(owners[gx])]
    return peer, pool, parts


def rank_program(g, core, T, topo):
    rank = T.rank_of(core)
    if rank is None:
        return
    S, cores = T.sem, T.cores
    row, col = rank // GC, rank % GC
    peer, pool, parts = _plan(rank, cores, topo)
    mine, off = (col * CH) // NC, (col * CH) % NC
    products = ((row, T.pl, T.sl, S.ml, S.cl), (GR - 1 - row, T.pc, T.sc, S.mc, S.cc))

    g.sync.dma_start(T.xb[:], T.x[:]).then_inc(S.lx, 16)
    g.sync.dma_start(T.wb[:], T.w[:]).then_inc(S.lw, 16)

    v = g.vector
    v.wait_ge(S.lx, 16)
    v.quantize_mx(T.xq[:], T.xs[:], T.xb[:]).then_inc(S.qx, 1)
    v.wait_ge(S.lw, 16)
    v.quantize_mx(T.wq[:], T.ws[:], T.wb[:]).then_inc(S.qw, 1)

    t = g.tensor
    t.wait_ge(S.qx, 1)
    t.wait_ge(S.qw, 1)
    t.matmul_mx(T.pl[:, 0:NC], T.wq[:], T.ws[:], T.xq[:], T.xs[:], True, True).then_inc(S.ml, 1)
    t.wait_ge(S.xa, 2 * len(_bits(_plan(peer, cores, topo)[1])))
    t.matmul_mx(T.pc[:, 0:NC], T.wq[:], T.ws[:], T.rq[:], T.rs[:], True, True).then_inc(S.mc, 1)

    sent = 0
    g.wait_ge(S.qx, 1)
    rid, pid = topo.addr(cores[peer], core)
    g.remote_dma(out_ap=T.rq[:].bitcast(dt.uint8), in_ap=T.xq[:].bitcast(dt.uint8), remote_sem=S.xa,
                 local_sem=S.sent, pid=pid, routing_id=rid, dma_engine_mask=pool)
    g.remote_dma(out_ap=T.rs[:], in_ap=T.xs[:], remote_sem=S.xa,
                 local_sem=S.sent, pid=pid, routing_id=rid, dma_engine_mask=pool)
    sent += 2 * len(_bits(pool))

    for gx, ps, sb, mm_done, cp_done in products:
        js = [j for _, j, _ in parts[gx]]
        lo, hi = min(js) * CH, (max(js) + 1) * CH
        v.wait_ge(mm_done, 1)
        v.tensor_copy(sb[:, lo:hi], ps[:, lo:hi]).then_inc(cp_done, 1)
        g.wait_ge(cp_done, 1)
        transfers = []
        for d, j, m in parts[gx]:
            slot = [c for c in range(GC) if c != d % GC].index(col)
            rid, pid = topo.addr(cores[d], core)
            transfers.append(RemoteDMATransfer(dst_ids=[DstId(rid=rid, pnc=pid)], dma_engine_mask=m,
                                               remote_sem=S["p%d" % slot], src=sb[:, j * CH:(j + 1) * CH],
                                               dst=T.land[:, slot * CH:(slot + 1) * CH]))
            sent += len(_bits(m))
        g.remote_dma_fused(transfers, local_sem=S.sent)

    def far(c):
        a = cores[row * GC + c]
        return (topo.host(a), topo.chip(a)) != (topo.host(core), topo.chip(core))

    others = [c for c in range(GC) if c != col]
    acc = (T.pl if mine == row else T.pc)[:, off:off + CH]
    for n, c in enumerate(sorted(others, key=far)):
        slot = others.index(c)
        m = [m for d, _, m in _plan(row * GC + c, cores, topo)[2][mine] if d == rank][0]
        v.wait_ge(S["p%d" % slot], len(_bits(m)))
        if n:
            v.wait_ge(S.va, n)
        v.tensor_tensor(T.yb[:], acc, T.land[:, slot * CH:(slot + 1) * CH], AluOpType.add).then_inc(S.va, 1)
        acc = T.yb[:]

    g.sync.wait_ge(S.va, len(others))
    g.sync.dma_start(T.y[:], T.yb[:]).then_inc(S.ly, 16)
    g.sync.wait_ge(S.ly, 16)
    g.wait_ge(S.sent, sent)
